import numpy as np, ml_dtypes
CORES = [6,14,30,38,62,70,86,94,102]
N = 9
R, NS, T = 4096, 256, 128
def entries(a): return a.T.reshape(-1)
def pack(v, P): return np.ascontiguousarray(np.asarray(v, np.int32).reshape(-1, P).T)
def lists(rng, how):
    I = rng.integers(0, N * R, NS)
    if how == "alike": I[:] = rng.integers(N * R)
    if how == "distinct": I = rng.permutation(N * R)[:NS]
    if how == "hotrank": I = R * int(rng.integers(N)) + rng.integers(0, R, NS)
    if how == "edge": I = R * rng.integers(0, N, NS) + np.where(rng.random(NS) < 0.5, 0, R - 1)
    if how == "sorted": I = np.sort(I)
    return {"neg": np.broadcast_to(pack(I, 16), (N, 16, NS // 16)).copy()}
def setup_inputs(rng):
    return dict({"h": rng.standard_normal((N, 128, T), dtype=np.float32).astype(ml_dtypes.bfloat16), "tab": (rng.standard_normal((N, 128, R), dtype=np.float32) / 8).astype(ml_dtypes.bfloat16)}, **lists(rng, "uniform"))
def setup_inputs_alike(rng):
    d = setup_inputs(rng); d.update(lists(rng, "alike"))
    for k in ("h", "tab"): d[k] = (d[k].astype(np.float32) * 1024.0).astype(d[k].dtype)
    return d
def setup_inputs_distinct(rng):
    d = setup_inputs(rng); d.update(lists(rng, "distinct"))
    for k in ("h", "tab"): d[k] = (d[k].astype(np.float32) * (1 / 1024.0)).astype(d[k].dtype)
    return d
def setup_inputs_edge(rng):
    d = setup_inputs(rng); d.update(lists(rng, "edge"))
    return d
def setup_inputs_hotrank(rng):
    d = setup_inputs(rng); d.update(lists(rng, "hotrank"))
    return d
def setup_inputs_sorted(rng):
    d = setup_inputs(rng); d.update(lists(rng, "sorted"))
    return d
def check_inputs(x):
    bad = []
    if x["neg"].min() < 0 or x["neg"].max() >= N * R: bad.append("neg out of range")
    if not all(np.array_equal(a, x["neg"][0]) for a in x["neg"]): bad.append("neg isn't alike on all ranks")
    return bad
def reference(h, tab, neg):
    A = np.concatenate(list(tab), axis=1).astype(np.float64)
    S = A[:, entries(neg[0])]
    return {"y": np.stack([h[r].astype(np.float64).T @ S for r in range(N)]).astype(ml_dtypes.bfloat16)}

@@ -1,0 +1,144 @@
+from concourse.bass import DstId, RemoteDMATransfer
+from concourse.mybir import AluOpType, ActivationFunctionType
+
+N, R, NS = 9, 4096, 256
+G1 = 3
+G2 = N // G1
+Z = 8
+H = NS // 2
+WT = Z + R + Z
+WR = Z + G1 * NS + Z
+
+SCRATCH = {
+    "tabw": ("sbuf", [128, WT], "bfloat16"),
+    "hs": ("sbuf", [128, 128], "bfloat16"),
+    "negs": ("sbuf", [128, 16], "int32"),
+    "jt": ("sbuf", [128, 16], "int32"),
+    "ow": ("sbuf", [128, 16], "int32"),
+    "tt": ("sbuf", [128, 16], "int32"),
+    "cat": ("sbuf", [128, 32], "float32"),
+    "ones": ("sbuf", [128, 128], "float32"),
+    "rep": ("sbuf", [128, 128], "float32"),
+    "off": ("sbuf", [128, 32], "uint16"),
+    "row": ("sbuf", [128, WR], "bfloat16"),
+    "col": ("sbuf", [128, G2 * NS], "bfloat16"),
+    "ys": ("sbuf", [128, NS], "bfloat16"),
+    "prep": ("psum", [128, 512], "float32"),
+    "acc0": ("psum", [128, 512], "float32"),
+    "acc1": ("psum", [128, 512], "float32"),
+}
+SEMAPHORES = ["ldn", "ldt", "ldh", "st", "s_ones", "s_z", "s_j", "s_rep", "s_cat", "s_b", "s_c", "s_p", "s_off",
+              "s_g", "s_m", "mm0", "mm1", "cp", "arr1", "sent"] + ["arr2_%d" % k for k in range(G2)]
+
+
+def rank_program(g, core, T, topo):
+    r = T.rank_of(core)
+    if r is None:
+        return
+    S = T.sem
+    v, a, pe, sy = g.vector, g.scalar, g.tensor, g.sync
+    Copy = ActivationFunctionType.Copy
+    i, s = divmod(r, G1)
+
+    def row_of(c):
+        q = T.rank_of(c)
+        return [T.cores[q // G1 * G1 + k] for k in range(G1) if k != q % G1]
+
+    def col_of(c):
+        q = T.rank_of(c)
+        return [T.cores[k * G1 + q % G1] for k in range(G2) if k != q // G1]
+
+    def engines(src, dsts):
+        m = topo.mask(src, dsts[0])
+        for d in dsts:
+            if not topo.may_write(src, d):
+                raise ValueError("core %d may not write to core %d" % (src, d))
+            m &= topo.mask(src, d)
+        return m
+
+    def count(m):
+        return bin(m).count("1")
+
+    def send(ap, dsts, sem):
+        ids = [DstId(rid=topo.addr(d)[0], pnc=topo.addr(d)[1]) for d in dsts]
+        m = engines(core, dsts)
+        g.remote_dma_fused([RemoteDMATransfer(dst_ids=ids, dma_engine_mask=m, remote_sem=sem, srcs=[ap],
+                                              dsts=[ap for _ in dsts], alu_op=0)], local_sem=S.sent)
+        return count(m)
+
+    own = Z + s * NS
+    mine = i * NS
+
+    sy.dma_start(T.negs[0:16, :], T.neg[:]).then_inc(S.ldn, 16)
+    sy.dma_start(T.tabw[:, Z:Z + R], T.tab[:]).then_inc(S.ldt, 16)
+    sy.dma_start(T.hs[:], T.h[:]).then_inc(S.ldh, 16)
+
+    g.iota(T.jt[0:16, :], [[16, 16]], Z - NS * G1 * i, 1).then_inc(S.s_j, 1)
+    g.wait_ge(S.s_ones, 1)
+    g.affine_select(T.rep[0:16, :], T.ones[0:16, :], [[0, 8], [1, 16]], AluOpType.is_equal, 0.0, 0, -1).then_inc(S.s_rep, 1)
+
+    v.memset(T.ones[0:16, :], 1.0).then_inc(S.s_ones, 1)
+    v.memset(T.tabw[:, 0:Z], 0.0).then_inc(S.s_z, 1)
+    v.memset(T.tabw[:, Z + R:WT], 0.0).then_inc(S.s_z, 1)
+    v.memset(T.row[:, 0:Z], 0.0).then_inc(S.s_z, 1)
+    v.memset(T.row[:, WR - Z:WR], 0.0).then_inc(S.s_z, 1)
+    v.wait_ge(S.ldn, 16)
+    v.tensor_scalar(T.cat[0:16, 0:16], T.negs[0:16, :], Z - R * r, Z + R, AluOpType.add, AluOpType.min).then_inc(S.s_cat, 1)
+    v.tensor_scalar(T.ow[0:16, :], T.negs[0:16, :], 4, 0xFFFF00, AluOpType.arith_shift_right,
+                    AluOpType.bitwise_and).then_inc(S.s_b, 1)
+    v.wait_ge(S.s_b, 1)
+    v.wait_ge(S.s_j, 1)
+    v.tensor_tensor(T.tt[0:16, :], T.ow[0:16, :], T.jt[0:16, :], AluOpType.add).then_inc(S.s_c, 1)
+    v.wait_ge(S.s_c, 1)
+    v.tensor_scalar(T.cat[0:16, 16:32], T.tt[0:16, :], Z + G1 * NS, None, AluOpType.min).then_inc(S.s_cat, 1)
+
+    pe.wait_ge(S.s_rep, 1)
+    pe.wait_ge(S.s_cat, 2)
+    pe.matmul(T.prep[:, 0:32], T.rep[0:16, :], T.cat[0:16, :], True, True).then_inc(S.s_p, 1)
+    v.wait_ge(S.s_p, 1)
+    v.tensor_copy(T.off[:], T.prep[:, 0:32]).then_inc(S.s_off, 1)
+
+    for q in (v, a):
+        q.wait_ge(S.s_off, 1)
+        q.wait_ge(S.s_z, 4)
+        q.wait_ge(S.ldt, 16)
+    v.tensor_copy(T.row[:, own:own + H], T.tabw[:, 0:WT].indirect(T.off[:, 0:8])).then_inc(S.s_g, 1)
+    a.activation(T.row[:, own + H:own + NS], T.tabw[:, 0:WT].indirect(T.off[:, 8:16]), Copy).then_inc(S.s_g, 1)
+
+    g.wait_ge(S.s_g, 2)
+    left = send(T.row[:, own:own + NS], row_of(core), S.arr1)
+
+    need = sum(count(engines(p, row_of(p))) for p in row_of(core))
+    for q in (v, a):
+        q.wait_ge(S.s_g, 2)
+        q.wait_ge(S.arr1, need)
+    v.tensor_copy(T.col[:, mine:mine + H], T.row[:, 0:WR].indirect(T.off[:, 16:24])).then_inc(S.s_m, 1)
+    a.activation(T.col[:, mine + H:mine + NS], T.row[:, 0:WR].indirect(T.off[:, 24:32]), Copy).then_inc(S.s_m, 1)
+
+    g.wait_ge(S.s_m, 2)
+    if G2 > 1:
+        left += send(T.col[:, mine:mine + NS], col_of(core), S["arr2_%d" % i])
+    g.wait_ge(S.sent, left)
+
+    order = [i] + [(i + k) % G2 for k in range(1, G2)]
+    pe.wait_ge(S.ldh, 16)
+    for n, k in enumerate(order):
+        if k == i:
+            pe.wait_ge(S.s_m, 2)
+        else:
+            p = T.cores[k * G1 + s]
+            pe.wait_ge(S["arr2_%d" % k], count(engines(p, col_of(p))))
+        first, last = n == 0, n == G2 - 1
+        m0 = pe.matmul(T.acc0[:, 0:H], T.hs[:], T.col[:, k * NS:k * NS + H], first, last)
+        m1 = pe.matmul(T.acc1[:, 0:H], T.hs[:], T.col[:, k * NS + H:(k + 1) * NS], first, last)
+        if last:
+            m0.then_inc(S.mm0, 1)
+            m1.then_inc(S.mm1, 1)
+
+    v.wait_ge(S.mm0, 1)
+    v.tensor_copy(T.ys[:, 0:H], T.acc0[:, 0:H]).then_inc(S.cp, 1)
+    a.wait_ge(S.mm1, 1)
+    a.activation(T.ys[:, H:NS], T.acc1[:, 0:H], Copy).then_inc(S.cp, 1)
+    sy.wait_ge(S.cp, 2)
+    sy.dma_start(T.y[:], T.ys[:]).then_inc(S.st, 16)
+    sy.wait_ge(S.st, 16)

@@ -6,8 +6,9 @@ G1 = 3
 G2 = N // G1
 Z = 8
 H = NS // 2
+Q = H // 2
 WT = Z + R + Z
-WR = Z + G1 * NS + Z
+WR = Z + G1 * H + Z
 
 SCRATCH = {
     "tabw": ("sbuf", [128, WT], "bfloat16"),
@@ -16,19 +17,25 @@ SCRATCH = {
     "jt": ("sbuf", [128, 16], "int32"),
     "ow": ("sbuf", [128, 16], "int32"),
     "tt": ("sbuf", [128, 16], "int32"),
-    "cat": ("sbuf", [128, 32], "float32"),
+    "cat": ("sbuf", [128, 16], "float32"),
+    "cat2": ("sbuf", [128, 16], "float32"),
     "ones": ("sbuf", [128, 128], "float32"),
     "rep": ("sbuf", [128, 128], "float32"),
-    "off": ("sbuf", [128, 32], "uint16"),
-    "row": ("sbuf", [128, WR], "bfloat16"),
-    "col": ("sbuf", [128, G2 * NS], "bfloat16"),
+    "off": ("sbuf", [128, 16], "uint16"),
+    "off2": ("sbuf", [128, 16], "uint16"),
+    "row0": ("sbuf", [128, WR], "bfloat16"),
+    "row1": ("sbuf", [128, WR], "bfloat16"),
+    "col0": ("sbuf", [128, G2 * H], "bfloat16"),
+    "col1": ("sbuf", [128, G2 * H], "bfloat16"),
     "ys": ("sbuf", [128, NS], "bfloat16"),
     "prep": ("psum", [128, 512], "float32"),
+    "prep2": ("psum", [128, 512], "float32"),
     "acc0": ("psum", [128, 512], "float32"),
     "acc1": ("psum", [128, 512], "float32"),
 }
-SEMAPHORES = ["ldn", "ldt", "ldh", "st", "s_ones", "s_z", "s_j", "s_rep", "s_cat", "s_b", "s_c", "s_p", "s_off",
-              "s_g", "s_m", "mm0", "mm1", "cp", "arr1", "sent"] + ["arr2_%d" % k for k in range(G2)]
+SEMAPHORES = ["ldn", "ldt", "ldh", "st", "s_ones", "s_z", "s_j", "s_rep", "s_c1", "s_c2", "s_b", "s_c", "s_p1", "s_p2",
+              "s_off", "s_off2", "s_g0", "s_g1", "s_m0", "s_m1", "mm0", "mm1", "cp", "arr1_0", "arr1_1", "sent"]
+SEMAPHORES += ["arr2_%d_%d" % (e, k) for e in range(2) for k in range(G2)]
 
 
 def rank_program(g, core, T, topo):
@@ -66,74 +73,88 @@ def rank_program(g, core, T, topo):
                                               dsts=[ap for _ in dsts], alu_op=0)], local_sem=S.sent)
         return count(m)
 
-    own = Z + s * NS
-    mine = i * NS
+    own = Z + s * H
+    mine = i * H
+    row = [T.row0, T.row1]
+    col = [T.col0, T.col1]
+    acc = [T.acc0, T.acc1]
 
     sy.dma_start(T.negs[0:16, :], T.neg[:]).then_inc(S.ldn, 16)
     sy.dma_start(T.tabw[:, Z:Z + R], T.tab[:]).then_inc(S.ldt, 16)
     sy.dma_start(T.hs[:], T.h[:]).then_inc(S.ldh, 16)
 
-    g.iota(T.jt[0:16, :], [[16, 16]], Z - NS * G1 * i, 1).then_inc(S.s_j, 1)
     g.wait_ge(S.s_ones, 1)
     g.affine_select(T.rep[0:16, :], T.ones[0:16, :], [[0, 8], [1, 16]], AluOpType.is_equal, 0.0, 0, -1).then_inc(S.s_rep, 1)
+    g.iota(T.jt[0:16, :], [[0, 2], [16, 8]], Z - H * G1 * i, 1).then_inc(S.s_j, 1)
 
     v.memset(T.ones[0:16, :], 1.0).then_inc(S.s_ones, 1)
     v.memset(T.tabw[:, 0:Z], 0.0).then_inc(S.s_z, 1)
     v.memset(T.tabw[:, Z + R:WT], 0.0).then_inc(S.s_z, 1)
-    v.memset(T.row[:, 0:Z], 0.0).then_inc(S.s_z, 1)
-    v.memset(T.row[:, WR - Z:WR], 0.0).then_inc(S.s_z, 1)
+    for e in range(2):
+        v.memset(row[e][:, 0:Z], 0.0).then_inc(S.s_z, 1)
+        v.memset(row[e][:, WR - Z:WR], 0.0).then_inc(S.s_z, 1)
     v.wait_ge(S.ldn, 16)
-    v.tensor_scalar(T.cat[0:16, 0:16], T.negs[0:16, :], Z - R * r, Z + R, AluOpType.add, AluOpType.min).then_inc(S.s_cat, 1)
-    v.tensor_scalar(T.ow[0:16, :], T.negs[0:16, :], 4, 0xFFFF00, AluOpType.arith_shift_right,
+    v.tensor_scalar(T.cat[0:16, :], T.negs[0:16, :], Z - R * r, Z + R, AluOpType.add, AluOpType.min).then_inc(S.s_c1, 1)
+    v.tensor_scalar(T.ow[0:16, :], T.negs[0:16, :], 5, 0xFFFF80, AluOpType.arith_shift_right,
                     AluOpType.bitwise_and).then_inc(S.s_b, 1)
     v.wait_ge(S.s_b, 1)
     v.wait_ge(S.s_j, 1)
     v.tensor_tensor(T.tt[0:16, :], T.ow[0:16, :], T.jt[0:16, :], AluOpType.add).then_inc(S.s_c, 1)
     v.wait_ge(S.s_c, 1)
-    v.tensor_scalar(T.cat[0:16, 16:32], T.tt[0:16, :], Z + G1 * NS, None, AluOpType.min).then_inc(S.s_cat, 1)
+    v.tensor_scalar(T.cat2[0:16, :], T.tt[0:16, :], Z + G1 * H, None, AluOpType.min).then_inc(S.s_c2, 1)
 
     pe.wait_ge(S.s_rep, 1)
-    pe.wait_ge(S.s_cat, 2)
-    pe.matmul(T.prep[:, 0:32], T.rep[0:16, :], T.cat[0:16, :], True, True).then_inc(S.s_p, 1)
-    v.wait_ge(S.s_p, 1)
-    v.tensor_copy(T.off[:], T.prep[:, 0:32]).then_inc(S.s_off, 1)
+    pe.wait_ge(S.s_c1, 1)
+    pe.matmul(T.prep[:, 0:16], T.rep[0:16, :], T.cat[0:16, :], True, True).then_inc(S.s_p1, 1)
+    pe.wait_ge(S.s_c2, 1)
+    pe.matmul(T.prep2[:, 0:16], T.rep[0:16, :], T.cat2[0:16, :], True, True).then_inc(S.s_p2, 1)
+    v.wait_ge(S.s_p1, 1)
+    v.tensor_copy(T.off[:], T.prep[:, 0:16]).then_inc(S.s_off, 1)
 
     for q in (v, a):
         q.wait_ge(S.s_off, 1)
-        q.wait_ge(S.s_z, 4)
+        q.wait_ge(S.s_z, 6)
         q.wait_ge(S.ldt, 16)
-    v.tensor_copy(T.row[:, own:own + H], T.tabw[:, 0:WT].indirect(T.off[:, 0:8])).then_inc(S.s_g, 1)
-    a.activation(T.row[:, own + H:own + NS], T.tabw[:, 0:WT].indirect(T.off[:, 8:16]), Copy).then_inc(S.s_g, 1)
+    v.tensor_copy(T.row0[:, own:own + H], T.tabw[:, 0:WT].indirect(T.off[:, 0:8])).then_inc(S.s_g0, 1)
+    a.activation(T.row1[:, own:own + H], T.tabw[:, 0:WT].indirect(T.off[:, 8:16]), Copy).then_inc(S.s_g1, 1)
+    v.wait_ge(S.s_p2, 1)
+    v.tensor_copy(T.off2[:], T.prep2[:, 0:16]).then_inc(S.s_off2, 1)
 
-    g.wait_ge(S.s_g, 2)
-    left = send(T.row[:, own:own + NS], row_of(core), S.arr1)
+    left = 0
+    for e in range(2):
+        g.wait_ge(S["s_g%d" % e], 1)
+        left += send(row[e][:, own:own + H], row_of(core), S["arr1_%d" % e])
 
     need = sum(count(engines(p, row_of(p))) for p in row_of(core))
     for q in (v, a):
-        q.wait_ge(S.s_g, 2)
-        q.wait_ge(S.arr1, need)
-    v.tensor_copy(T.col[:, mine:mine + H], T.row[:, 0:WR].indirect(T.off[:, 16:24])).then_inc(S.s_m, 1)
-    a.activation(T.col[:, mine + H:mine + NS], T.row[:, 0:WR].indirect(T.off[:, 24:32]), Copy).then_inc(S.s_m, 1)
+        q.wait_ge(S.s_off2, 1)
+    for e in range(2):
+        for q in (v, a):
+            q.wait_ge(S["s_g%d" % e], 1)
+            q.wait_ge(S["arr1_%d" % e], need)
+        v.tensor_copy(col[e][:, mine:mine + Q],
+                      row[e][:, 0:WR].indirect(T.off2[:, 8 * e:8 * e + 4])).then_inc(S["s_m%d" % e], 1)
+        a.activation(col[e][:, mine + Q:mine + H],
+                     row[e][:, 0:WR].indirect(T.off2[:, 8 * e + 4:8 * e + 8]), Copy).then_inc(S["s_m%d" % e], 1)
 
-    g.wait_ge(S.s_m, 2)
-    if G2 > 1:
-        left += send(T.col[:, mine:mine + NS], col_of(core), S["arr2_%d" % i])
+    for e in range(2):
+        g.wait_ge(S["s_m%d" % e], 2)
+        left += send(col[e][:, mine:mine + H], col_of(core), S["arr2_%d_%d" % (e, i)])
     g.wait_ge(S.sent, left)
 
-    order = [i] + [(i + k) % G2 for k in range(1, G2)]
+    others = [(i + k) % G2 for k in range(1, G2)]
     pe.wait_ge(S.ldh, 16)
-    for n, k in enumerate(order):
-        if k == i:
-            pe.wait_ge(S.s_m, 2)
-        else:
+    for e in range(2):
+        pe.wait_ge(S["s_m%d" % e], 2)
+        pe.matmul(acc[e][:, 0:H], T.hs[:], col[e][:, mine:mine + H], True, False)
+    for e in range(2):
+        for n, k in enumerate(others):
             p = T.cores[k * G1 + s]
-            pe.wait_ge(S["arr2_%d" % k], count(engines(p, col_of(p))))
-        first, last = n == 0, n == G2 - 1
-        m0 = pe.matmul(T.acc0[:, 0:H], T.hs[:], T.col[:, k * NS:k * NS + H], first, last)
-        m1 = pe.matmul(T.acc1[:, 0:H], T.hs[:], T.col[:, k * NS + H:(k + 1) * NS], first, last)
-        if last:
-            m0.then_inc(S.mm0, 1)
-            m1.then_inc(S.mm1, 1)
+            pe.wait_ge(S["arr2_%d_%d" % (e, k)], count(engines(p, col_of(p))))
+            last = n == len(others) - 1
+            m = pe.matmul(acc[e][:, 0:H], T.hs[:], col[e][:, k * H:(k + 1) * H], False, last)
+            if last:
+                m.then_inc(S["mm%d" % e], 1)
 
     v.wait_ge(S.mm0, 1)
     v.tensor_copy(T.ys[:, 0:H], T.acc0[:, 0:H]).then_inc(S.cp, 1)

from concourse.bass import DstId, RemoteDMATransfer
from concourse.mybir import AluOpType, ActivationFunctionType

N, R, NS = 9, 4096, 256
G1 = 3
G2 = N // G1
Z = 8
H = NS // 2
Q = H // 2
WT = Z + R + Z
WR = Z + G1 * H + Z

SCRATCH = {
    "tabw": ("sbuf", [128, WT], "bfloat16"),
    "hs": ("sbuf", [128, 128], "bfloat16"),
    "negs": ("sbuf", [128, 16], "int32"),
    "jt": ("sbuf", [128, 16], "int32"),
    "ow": ("sbuf", [128, 16], "int32"),
    "tt": ("sbuf", [128, 16], "int32"),
    "cat": ("sbuf", [128, 16], "float32"),
    "cat2": ("sbuf", [128, 16], "float32"),
    "ones": ("sbuf", [128, 128], "float32"),
    "rep": ("sbuf", [128, 128], "float32"),
    "off": ("sbuf", [128, 16], "uint16"),
    "off2": ("sbuf", [128, 16], "uint16"),
    "row0": ("sbuf", [128, WR], "bfloat16"),
    "row1": ("sbuf", [128, WR], "bfloat16"),
    "col0": ("sbuf", [128, G2 * H], "bfloat16"),
    "col1": ("sbuf", [128, G2 * H], "bfloat16"),
    "ys": ("sbuf", [128, NS], "bfloat16"),
    "prep": ("psum", [128, 512], "float32"),
    "prep2": ("psum", [128, 512], "float32"),
    "acc0": ("psum", [128, 512], "float32"),
    "acc1": ("psum", [128, 512], "float32"),
}
SEMAPHORES = ["ldn", "ldt", "ldh", "st", "s_ones", "s_z", "s_j", "s_rep", "s_c1", "s_c2", "s_b", "s_c", "s_p1", "s_p2",
              "s_off", "s_off2", "s_g0", "s_g1", "s_m0", "s_m1", "mm0", "mm1", "cp", "arr1_0", "arr1_1", "sent"]
SEMAPHORES += ["arr2_%d_%d" % (e, k) for e in range(2) for k in range(G2)]


def rank_program(g, core, T, topo):
    r = T.rank_of(core)
    if r is None:
        return
    S = T.sem
    v, a, pe, sy = g.vector, g.scalar, g.tensor, g.sync
    Copy = ActivationFunctionType.Copy
    i, s = divmod(r, G1)

    def row_of(c):
        q = T.rank_of(c)
        return [T.cores[q // G1 * G1 + k] for k in range(G1) if k != q % G1]

    def col_of(c):
        q = T.rank_of(c)
        return [T.cores[k * G1 + q % G1] for k in range(G2) if k != q // G1]

    def engines(src, dsts):
        m = topo.mask(src, dsts[0])
        for d in dsts:
            if not topo.may_write(src, d):
                raise ValueError("core %d may not write to core %d" % (src, d))
            m &= topo.mask(src, d)
        return m

    def count(m):
        return bin(m).count("1")

    def send(ap, dsts, sem):
        ids = [DstId(rid=topo.addr(d)[0], pnc=topo.addr(d)[1]) for d in dsts]
        m = engines(core, dsts)
        g.remote_dma_fused([RemoteDMATransfer(dst_ids=ids, dma_engine_mask=m, remote_sem=sem, srcs=[ap],
                                              dsts=[ap for _ in dsts], alu_op=0)], local_sem=S.sent)
        return count(m)

    own = Z + s * H
    mine = i * H
    row = [T.row0, T.row1]
    col = [T.col0, T.col1]
    acc = [T.acc0, T.acc1]

    sy.dma_start(T.negs[0:16, :], T.neg[:]).then_inc(S.ldn, 16)
    sy.dma_start(T.tabw[:, Z:Z + R], T.tab[:]).then_inc(S.ldt, 16)
    sy.dma_start(T.hs[:], T.h[:]).then_inc(S.ldh, 16)

    g.wait_ge(S.s_ones, 1)
    g.affine_select(T.rep[0:16, :], T.ones[0:16, :], [[0, 8], [1, 16]], AluOpType.is_equal, 0.0, 0, -1).then_inc(S.s_rep, 1)
    g.iota(T.jt[0:16, :], [[0, 2], [16, 8]], Z - H * G1 * i, 1).then_inc(S.s_j, 1)

    v.memset(T.ones[0:16, :], 1.0).then_inc(S.s_ones, 1)
    v.memset(T.tabw[:, 0:Z], 0.0).then_inc(S.s_z, 1)
    v.memset(T.tabw[:, Z + R:WT], 0.0).then_inc(S.s_z, 1)
    for e in range(2):
        v.memset(row[e][:, 0:Z], 0.0).then_inc(S.s_z, 1)
        v.memset(row[e][:, WR - Z:WR], 0.0).then_inc(S.s_z, 1)
    v.wait_ge(S.ldn, 16)
    v.tensor_scalar(T.cat[0:16, :], T.negs[0:16, :], Z - R * r, Z + R, AluOpType.add, AluOpType.min).then_inc(S.s_c1, 1)
    v.tensor_scalar(T.ow[0:16, :], T.negs[0:16, :], 5, 0xFFFF80, AluOpType.arith_shift_right,
                    AluOpType.bitwise_and).then_inc(S.s_b, 1)
    v.wait_ge(S.s_b, 1)
    v.wait_ge(S.s_j, 1)
    v.tensor_tensor(T.tt[0:16, :], T.ow[0:16, :], T.jt[0:16, :], AluOpType.add).then_inc(S.s_c, 1)
    v.wait_ge(S.s_c, 1)
    v.tensor_scalar(T.cat2[0:16, :], T.tt[0:16, :], Z + G1 * H, None, AluOpType.min).then_inc(S.s_c2, 1)

    pe.wait_ge(S.s_rep, 1)
    pe.wait_ge(S.s_c1, 1)
    pe.matmul(T.prep[:, 0:16], T.rep[0:16, :], T.cat[0:16, :], True, True).then_inc(S.s_p1, 1)
    pe.wait_ge(S.s_c2, 1)
    pe.matmul(T.prep2[:, 0:16], T.rep[0:16, :], T.cat2[0:16, :], True, True).then_inc(S.s_p2, 1)
    v.wait_ge(S.s_p1, 1)
    v.tensor_copy(T.off[:], T.prep[:, 0:16]).then_inc(S.s_off, 1)

    for q in (v, a):
        q.wait_ge(S.s_off, 1)
        q.wait_ge(S.s_z, 6)
        q.wait_ge(S.ldt, 16)
    v.tensor_copy(T.row0[:, own:own + H], T.tabw[:, 0:WT].indirect(T.off[:, 0:8])).then_inc(S.s_g0, 1)
    a.activation(T.row1[:, own:own + H], T.tabw[:, 0:WT].indirect(T.off[:, 8:16]), Copy).then_inc(S.s_g1, 1)
    v.wait_ge(S.s_p2, 1)
    v.tensor_copy(T.off2[:], T.prep2[:, 0:16]).then_inc(S.s_off2, 1)

    left = 0
    for e in range(2):
        g.wait_ge(S["s_g%d" % e], 1)
        left += send(row[e][:, own:own + H], row_of(core), S["arr1_%d" % e])

    need = sum(count(engines(p, row_of(p))) for p in row_of(core))
    for q in (v, a):
        q.wait_ge(S.s_off2, 1)
    for e in range(2):
        for q in (v, a):
            q.wait_ge(S["s_g%d" % e], 1)
            q.wait_ge(S["arr1_%d" % e], need)
        v.tensor_copy(col[e][:, mine:mine + Q],
                      row[e][:, 0:WR].indirect(T.off2[:, 8 * e:8 * e + 4])).then_inc(S["s_m%d" % e], 1)
        a.activation(col[e][:, mine + Q:mine + H],
                     row[e][:, 0:WR].indirect(T.off2[:, 8 * e + 4:8 * e + 8]), Copy).then_inc(S["s_m%d" % e], 1)

    for e in range(2):
        g.wait_ge(S["s_m%d" % e], 2)
        left += send(col[e][:, mine:mine + H], col_of(core), S["arr2_%d_%d" % (e, i)])
    g.wait_ge(S.sent, left)

    others = [(i + k) % G2 for k in range(1, G2)]
    pe.wait_ge(S.ldh, 16)
    for e in range(2):
        pe.wait_ge(S["s_m%d" % e], 2)
        pe.matmul(acc[e][:, 0:H], T.hs[:], col[e][:, mine:mine + H], True, False)
    for e in range(2):
        for n, k in enumerate(others):
            p = T.cores[k * G1 + s]
            pe.wait_ge(S["arr2_%d_%d" % (e, k)], count(engines(p, col_of(p))))
            last = n == len(others) - 1
            m = pe.matmul(acc[e][:, 0:H], T.hs[:], col[e][:, k * H:(k + 1) * H], False, last)
            if last:
                m.then_inc(S["mm%d" % e], 1)

    v.wait_ge(S.mm0, 1)
    v.tensor_copy(T.ys[:, 0:H], T.acc0[:, 0:H]).then_inc(S.cp, 1)
    a.wait_ge(S.mm1, 1)
    a.activation(T.ys[:, H:NS], T.acc1[:, 0:H], Copy).then_inc(S.cp, 1)
    sy.wait_ge(S.cp, 2)
    sy.dma_start(T.y[:], T.ys[:]).then_inc(S.st, 16)
    sy.wait_ge(S.st, 16)
